import numpy as np
CORES = [2,3,6,7,58,59,62,63,114,115,118,119]
N = 12
F = 64
BOUND = 15664.2
def setup_inputs(rng):
    gr = rng.standard_normal((1, 128, N * F), dtype=np.float32) + rng.standard_normal((N, 128, N * F), dtype=np.float32)
    return {"gr": gr}
def setup_inputs_big(rng):
    d = setup_inputs(rng)
    for k in ("gr",): d[k] = (d[k].astype(np.float32) * 1024.0).astype(d[k].dtype)
    return d
def setup_inputs_small(rng):
    d = setup_inputs(rng)
    for k in ("gr",): d[k] = (d[k].astype(np.float32) * (1 / 1024.0)).astype(d[k].dtype)
    return d
def setup_inputs_apart(rng):
    d = setup_inputs(rng)
    f = (10.0 ** rng.permutation(np.linspace(-1.5, 1.5, N))).astype(np.float32).reshape(N, 1, 1)
    for k in ("gr",): d[k] = (d[k].astype(np.float32) * f).astype(d[k].dtype)
    return d
def setup_inputs_far(rng):
    d = setup_inputs(rng)
    for k in ("gr",): d[k] = (d[k].astype(np.float32) * 16384.0).astype(d[k].dtype)
    return d
def setup_inputs_over(rng):
    d = setup_inputs(rng)
    f = np.float32(10.0 ** rng.uniform(1.5, 3.5)) * np.where(rng.random((1, 128, N * F)) < 0.5, 0.1, 1.0).astype(np.float32)
    for k in ("gr",): d[k] = (d[k].astype(np.float32) * f).astype(d[k].dtype)
    return d
def reference(gr):
    s = gr.astype(np.float64).sum(axis=0)
    nrm = np.sqrt((s ** 2).sum())
    s = s * min(1.0, BOUND / nrm)
    return {"y": np.stack([s[:, F * r:F * r + F] for r in range(N)]).astype(np.float32)}

@@ -1,0 +1,253 @@
+import math
+from concourse.bass import DstId, RemoteDMATransfer
+from concourse.mybir import AluOpType, ActivationFunctionType
+
+F = 64
+S3_FLAT = True
+
+SCRATCH = {
+    "x": ("sbuf", [128, 768], "float32"),
+    "l1": ("sbuf", [128, 384], "float32"),
+    "lb": ("sbuf", [128, 192], "float32"),
+    "l2": ("sbuf", [128, 128], "float32"),
+    "r1": ("sbuf", [128, 128], "float32"),
+    "s": ("sbuf", [128, 64], "float32"),
+    "sqj": ("sbuf", [128, 64], "float32"),
+    "qown": ("sbuf", [128, 4], "float32"),
+    "qland": ("sbuf", [128, 12], "float32"),
+    "qland2": ("sbuf", [128, 4], "float32"),
+    "qchip": ("sbuf", [128, 4], "float32"),
+    "zr": ("sbuf", [128, 4], "float32"),
+    "ones": ("sbuf", [128, 128], "float32"),
+    "flr": ("sbuf", [128, 12], "float32"),
+    "scn": ("sbuf", [128, 12], "float32"),
+    "z": ("sbuf", [128, 4], "float32"),
+    "rz": ("sbuf", [128, 4], "float32"),
+    "t": ("sbuf", [128, 4], "float32"),
+    "u": ("sbuf", [128, 4], "float32"),
+    "ysb": ("sbuf", [128, 64], "float32"),
+    "accA": ("psum", [128, 512], "float32"),
+    "accB": ("psum", [128, 512], "float32"),
+    "ps": ("psum", [128, 512], "float32"),
+}
+SEMAPHORES = ["ld0", "ld1", "ld2", "a1_0", "a1_1", "a1_2", "b1", "a2_0", "a2_1", "a3", "a4", "lsem",
+              "m_ones", "m_flr", "m_zr", "c_a", "c_b", "r1a", "r1b", "r1done", "bb0", "bb1", "bb2", "r2a", "sdone",
+              "sq", "qcs", "pe0", "pe1", "qc", "zs", "rzs", "ts", "us", "ydone", "st"]
+
+
+def _engines(mask):
+    return [e for e in range(mask.bit_length()) if (mask >> e) & 1]
+
+
+def _bits(es):
+    m = 0
+    for e in es:
+        m |= 1 << e
+    return m
+
+
+def rank_program(g, core, T, topo):
+    rank = T.rank_of(core)
+    if rank is None:
+        return
+    cores = list(T.cores)
+    n_ranks = len(cores)
+    sem = T.sem
+    add, mult, mx = AluOpType.add, AluOpType.mult, AluOpType.max
+
+    chips = []
+    for c in cores:
+        if topo.chip(c) not in chips:
+            chips.append(topo.chip(c))
+    members = {ch: [c for c in cores if topo.chip(c) == ch] for ch in chips}
+
+    def others(ch):
+        i = chips.index(ch)
+        return [chips[(i + k) % len(chips)] for k in range(1, len(chips))]
+
+    def siblings(c):
+        return [m for m in members[topo.chip(c)] if m != c]
+
+    def pair(c):
+        d = topo.die(c)
+        same = [m for m in members[topo.chip(c)] if topo.die(m) == d]
+        xch = others(topo.chip(c))[same.index(c)]
+        rs = [cores.index(m) for m in members[xch] if topo.die(m) == d]
+        assert len(rs) == 2 and rs[1] == rs[0] + 1
+        return rs
+
+    def group_cols(ch):
+        rs = [cores.index(m) for m in members[ch]]
+        assert rs == list(range(rs[0], rs[0] + len(rs)))
+        return F * rs[0], F * (rs[-1] + 1)
+
+    def dst_id(c):
+        assert topo.may_write(core, c)
+        rid, pid, _ = topo.addr(c)
+        return DstId(rid=rid, pnc=pid)
+
+    mychip = topo.chip(core)
+    sibs = siblings(core)
+    oth = others(mychip)
+    far = [c for c in cores if topo.chip(c) != mychip]
+    e_on = _engines(topo.mask(core, sibs[0]))
+    e_off = _engines(topo.mask(core, far[0]))
+    e_rest = [e for e in e_on if e not in e_off]
+    s1b_groups = [e_rest[0:4], e_rest[4:6], e_rest[6:8]]
+    mypair = pair(core)
+    pc0 = F * mypair[0]
+
+    lds = [sem.ld0, sem.ld1, sem.ld2]
+    a, b = group_cols(oth[0])
+    g.sync.dma_start(T.x[:, a:b], T.gr[:, a:b]).then_inc(sem.ld0, 16)
+    a, b = group_cols(oth[1])
+    g.scalar.dma_start(T.x[:, a:b], T.gr[:, a:b]).then_inc(sem.ld1, 16)
+    a, b = group_cols(mychip)
+    g.sync.dma_start(T.x[:, a:b], T.gr[:, a:b]).then_inc(sem.ld2, 16)
+
+    bound = float(T.tables["BOUND"])
+    sg = 2.0 ** -39
+    kk = sg * bound
+    floor = kk * kk
+    ncol = n_ranks if S3_FLAT else len(chips)
+    V = g.vector
+    V.memset(T.ones[:, :], 1.0).then_inc(sem.m_ones, 1)
+    V.memset(T.flr[:, 0:ncol - 1], 0.0).then_inc(sem.m_flr, 1)
+    V.memset(T.flr[:, ncol - 1:ncol], floor).then_inc(sem.m_flr, 1)
+    if not S3_FLAT:
+        V.memset(T.zr[:, :], 0.0).then_inc(sem.m_zr, 1)
+
+    lsem_total = 0
+
+    g.wait_ge(sem.ld0, 16)
+    g.wait_ge(sem.ld1, 16)
+    trs = []
+    for j, h in enumerate(sibs):
+        p0 = F * pair(h)[0]
+        slot = siblings(h).index(core)
+        es = e_on[4 * j:4 * j + 4]
+        trs.append(RemoteDMATransfer(dst_ids=[dst_id(h)], dma_engine_mask=_bits(es),
+                                     remote_sem=sem["a1_%d" % slot],
+                                     src=T.x[:, p0:p0 + 2 * F], dst=T.l1[:, 2 * F * slot:2 * F * (slot + 1)]))
+        lsem_total += len(es)
+    g.remote_dma_fused(trs, local_sem=sem.lsem)
+
+    g.wait_ge(sem.ld2, 16)
+    trs = []
+    for j, h in enumerate(sibs):
+        c0 = F * cores.index(h)
+        slot = siblings(h).index(core)
+        es = s1b_groups[j]
+        trs.append(RemoteDMATransfer(dst_ids=[dst_id(h)], dma_engine_mask=_bits(es), remote_sem=sem.b1,
+                                     src=T.x[:, c0:c0 + F], dst=T.lb[:, F * slot:F * (slot + 1)]))
+        lsem_total += len(es)
+    g.remote_dma_fused(trs, local_sem=sem.lsem)
+    b1_total = sum(len(s1b_groups[siblings(h).index(core)]) for h in sibs)
+
+    V.wait_ge(lds[oth.index(topo.chip(cores[mypair[0]]))], 16)
+    V.tensor_copy(T.accA[:, 0:2 * F], T.x[:, pc0:pc0 + 2 * F]).then_inc(sem.c_a, 1)
+    V.wait_ge(sem.ld2, 16)
+    V.tensor_copy(T.accB[:, 0:F], T.x[:, F * rank:F * (rank + 1)]).then_inc(sem.c_b, 1)
+    V.wait_ge(sem.c_a, 1)
+    V.wait_ge(sem.a1_0, 4)
+    V.tensor_tensor(T.accA[:, 0:2 * F], T.accA[:, 0:2 * F], T.l1[:, 0:2 * F], add).then_inc(sem.r1a, 1)
+    V.wait_ge(sem.r1a, 1)
+    V.wait_ge(sem.a1_1, 4)
+    V.tensor_tensor(T.accA[:, 0:2 * F], T.accA[:, 0:2 * F], T.l1[:, 2 * F:4 * F], add).then_inc(sem.r1b, 1)
+    V.wait_ge(sem.r1b, 1)
+    V.wait_ge(sem.a1_2, 4)
+    V.tensor_tensor(T.r1[:, :], T.accA[:, 0:2 * F], T.l1[:, 4 * F:6 * F], add).then_inc(sem.r1done, 1)
+
+    g.wait_ge(sem.r1done, 1)
+    trs = []
+    for j, r in enumerate(mypair):
+        o = cores[r]
+        slot = others(topo.chip(o)).index(mychip)
+        es = e_off[4 * j:4 * j + 4]
+        trs.append(RemoteDMATransfer(dst_ids=[dst_id(o)], dma_engine_mask=_bits(es),
+                                     remote_sem=sem["a2_%d" % slot],
+                                     src=T.r1[:, F * j:F * (j + 1)], dst=T.l2[:, F * slot:F * (slot + 1)]))
+        lsem_total += len(es)
+    g.remote_dma_fused(trs, local_sem=sem.lsem)
+
+    V.wait_ge(sem.c_b, 1)
+    V.wait_ge(sem.b1, b1_total)
+    prev = None
+    for k, sm in enumerate([sem.bb0, sem.bb1, sem.bb2]):
+        if prev is not None:
+            V.wait_ge(prev, 1)
+        V.tensor_tensor(T.accB[:, 0:F], T.accB[:, 0:F], T.lb[:, F * k:F * (k + 1)], add).then_inc(sm, 1)
+        prev = sm
+    V.wait_ge(sem.bb2, 1)
+    V.wait_ge(sem.a2_0, 4)
+    V.tensor_tensor(T.accB[:, 0:F], T.accB[:, 0:F], T.l2[:, 0:F], add).then_inc(sem.r2a, 1)
+    V.wait_ge(sem.r2a, 1)
+    V.wait_ge(sem.a2_1, 4)
+    V.tensor_tensor(T.s[:, :], T.accB[:, 0:F], T.l2[:, F:2 * F], add).then_inc(sem.sdone, 1)
+
+    g.scalar.wait_ge(sem.sdone, 1)
+    g.scalar.activation(T.sqj[:, :], T.s[:, :], ActivationFunctionType.Square, scale=sg,
+                        accum_out=T.qown[:, 0:1]).then_inc(sem.sq, 1)
+
+    P = g.tensor
+    g.wait_ge(sem.sq, 1)
+    if S3_FLAT:
+        def slot_at(c):
+            return (rank - cores.index(c) - 1) % n_ranks
+        trs = [RemoteDMATransfer(dst_ids=[dst_id(c) for c in far], dma_engine_mask=_bits(e_off), remote_sem=sem.a3,
+                                 srcs=[T.qown[:, 0:1]], dsts=[T.qland[:, slot_at(c):slot_at(c) + 1] for c in far]),
+               RemoteDMATransfer(dst_ids=[dst_id(c) for c in sibs], dma_engine_mask=_bits(e_rest), remote_sem=sem.a3,
+                                 srcs=[T.qown[:, 0:1]], dsts=[T.qland[:, slot_at(c):slot_at(c) + 1] for c in sibs])]
+        lsem_total += len(e_off) + len(e_rest)
+        g.remote_dma_fused(trs, local_sem=sem.lsem)
+        P.wait_ge(sem.m_ones, 1)
+        P.wait_ge(sem.sq, 1)
+        P.matmul(T.ps[:, 0:1], T.ones[:, :], T.qown[:, 0:1], True, True).then_inc(sem.pe0, 1)
+        P.wait_ge(sem.a3, len(e_off) * len(far) + len(e_rest) * len(sibs))
+        P.matmul(T.ps[:, 1:ncol], T.ones[:, :], T.qland[:, 0:ncol - 1], True, True).then_inc(sem.pe1, 1)
+    else:
+        ns = len(sibs)
+        trs = [RemoteDMATransfer(dst_ids=[dst_id(c) for c in sibs], dma_engine_mask=_bits(e_on), remote_sem=sem.a3,
+                                 srcs=[T.qown[:, 0:1]],
+                                 dsts=[T.qland[:, siblings(c).index(core):siblings(c).index(core) + 1] for c in sibs])]
+        lsem_total += len(e_on)
+        g.remote_dma_fused(trs, local_sem=sem.lsem)
+        V.wait_ge(sem.m_zr, 1)
+        V.wait_ge(sem.sq, 1)
+        V.wait_ge(sem.a3, len(e_on) * ns)
+        V.tensor_tensor_scan(T.qchip[:, 0:ns], T.qland[:, 0:ns], T.zr[:, 0:ns], T.qown[:, 0:1], add, add
+                             ).then_inc(sem.qcs, 1)
+        peers = [members[ch][members[mychip].index(core)] for ch in oth]
+        g.wait_ge(sem.qcs, 1)
+        trs = [RemoteDMATransfer(dst_ids=[dst_id(c) for c in peers], dma_engine_mask=_bits(e_off), remote_sem=sem.a4,
+                                 srcs=[T.qchip[:, ns - 1:ns]],
+                                 dsts=[T.qland2[:, others(topo.chip(c)).index(mychip):
+                                                others(topo.chip(c)).index(mychip) + 1] for c in peers])]
+        lsem_total += len(e_off)
+        g.remote_dma_fused(trs, local_sem=sem.lsem)
+        P.wait_ge(sem.m_ones, 1)
+        P.wait_ge(sem.qcs, 1)
+        P.matmul(T.ps[:, 0:1], T.ones[:, :], T.qchip[:, ns - 1:ns], True, True).then_inc(sem.pe0, 1)
+        P.wait_ge(sem.a4, len(e_off) * len(peers))
+        P.matmul(T.ps[:, 1:ncol], T.ones[:, :], T.qland2[:, 0:ncol - 1], True, True).then_inc(sem.pe1, 1)
+
+    V.wait_ge(sem.m_flr, 2)
+    V.wait_ge(sem.pe0, 1)
+    V.wait_ge(sem.pe1, 1)
+    V.tensor_tensor_scan(T.scn[:, 0:ncol], T.ps[:, 0:ncol], T.flr[:, 0:ncol], 0.0, add, mx).then_inc(sem.qc, 1)
+    qc = T.scn[:, ncol - 1:ncol]
+    g.scalar.wait_ge(sem.qc, 1)
+    g.scalar.activation(T.z[:, 0:1], qc, ActivationFunctionType.Sqrt).then_inc(sem.zs, 1)
+    V.wait_ge(sem.zs, 1)
+    V.reciprocal(T.rz[:, 0:1], T.z[:, 0:1]).then_inc(sem.rzs, 1)
+    V.wait_ge(sem.rzs, 1)
+    V.tensor_scalar(T.t[:, 0:1], T.rz[:, 0:1], T.rz[:, 0:1], qc, mult, mult).then_inc(sem.ts, 1)
+    V.wait_ge(sem.ts, 1)
+    V.tensor_scalar(T.u[:, 0:1], T.t[:, 0:1], -0.5 * kk, 1.5 * kk, mult, add).then_inc(sem.us, 1)
+    V.wait_ge(sem.us, 1)
+    V.tensor_scalar(T.ysb[:, :], T.s[:, :], T.rz[:, 0:1], T.u[:, 0:1], mult, mult).then_inc(sem.ydone, 1)
+
+    g.sync.wait_ge(sem.ydone, 1)
+    g.sync.dma_start(T.y[:, :], T.ysb[:, :]).then_inc(sem.st, 16)
+    g.sync.wait_ge(sem.st, 16)
+    g.wait_ge(sem.lsem, lsem_total)

@@ -1,38 +1,34 @@
-import math
 from concourse.bass import DstId, RemoteDMATransfer
 from concourse.mybir import AluOpType, ActivationFunctionType
 
 F = 64
-S3_FLAT = True
 
 SCRATCH = {
     "x": ("sbuf", [128, 768], "float32"),
     "l1": ("sbuf", [128, 384], "float32"),
     "lb": ("sbuf", [128, 192], "float32"),
     "l2": ("sbuf", [128, 128], "float32"),
+    "tb": ("sbuf", [128, 128], "float32"),
     "r1": ("sbuf", [128, 128], "float32"),
     "s": ("sbuf", [128, 64], "float32"),
     "sqj": ("sbuf", [128, 64], "float32"),
     "qown": ("sbuf", [128, 4], "float32"),
     "qland": ("sbuf", [128, 12], "float32"),
-    "qland2": ("sbuf", [128, 4], "float32"),
-    "qchip": ("sbuf", [128, 4], "float32"),
-    "zr": ("sbuf", [128, 4], "float32"),
     "ones": ("sbuf", [128, 128], "float32"),
     "flr": ("sbuf", [128, 12], "float32"),
     "scn": ("sbuf", [128, 12], "float32"),
-    "z": ("sbuf", [128, 4], "float32"),
-    "rz": ("sbuf", [128, 4], "float32"),
-    "t": ("sbuf", [128, 4], "float32"),
-    "u": ("sbuf", [128, 4], "float32"),
+    "rq": ("sbuf", [128, 4], "float32"),
+    "zb": ("sbuf", [128, 4], "float32"),
+    "d1": ("sbuf", [128, 4], "float32"),
+    "sc2": ("sbuf", [128, 4], "float32"),
     "ysb": ("sbuf", [128, 64], "float32"),
     "accA": ("psum", [128, 512], "float32"),
     "accB": ("psum", [128, 512], "float32"),
     "ps": ("psum", [128, 512], "float32"),
 }
-SEMAPHORES = ["ld0", "ld1", "ld2", "a1_0", "a1_1", "a1_2", "b1", "a2_0", "a2_1", "a3", "a4", "lsem",
-              "m_ones", "m_flr", "m_zr", "c_a", "c_b", "r1a", "r1b", "r1done", "bb0", "bb1", "bb2", "r2a", "sdone",
-              "sq", "qcs", "pe0", "pe1", "qc", "zs", "rzs", "ts", "us", "ydone", "st"]
+SEMAPHORES = ["ld0", "ld1", "ld2", "a1_0", "a1_1", "a1_2", "b1", "a2_0", "a2_1", "a3", "lsem",
+              "m_ones", "m_flr", "m_d1", "c_a", "c_b", "r1a", "r1b", "r1done", "bb0", "bb1", "bb2", "r2a", "sdone",
+              "sq", "pe0", "pe1", "qc", "zs", "rqs", "h1", "s2s", "ydone", "st"]
 
 
 def _engines(mask):
@@ -109,13 +105,14 @@ def rank_program(g, core, T, topo):
     sg = 2.0 ** -39
     kk = sg * bound
     floor = kk * kk
-    ncol = n_ranks if S3_FLAT else len(chips)
+    ncol = n_ranks
     V = g.vector
     V.memset(T.ones[:, :], 1.0).then_inc(sem.m_ones, 1)
     V.memset(T.flr[:, 0:ncol - 1], 0.0).then_inc(sem.m_flr, 1)
     V.memset(T.flr[:, ncol - 1:ncol], floor).then_inc(sem.m_flr, 1)
-    if not S3_FLAT:
-        V.memset(T.zr[:, :], 0.0).then_inc(sem.m_zr, 1)
+    V.memset(T.d1[:, 0:1], 0.0).then_inc(sem.m_d1, 1)
+    V.memset(T.d1[:, 1:2], 1.5).then_inc(sem.m_d1, 1)
+    V.memset(T.d1[:, 2:3], 0.0).then_inc(sem.m_d1, 1)
 
     lsem_total = 0
 
@@ -150,13 +147,13 @@ def rank_program(g, core, T, topo):
     V.tensor_copy(T.accB[:, 0:F], T.x[:, F * rank:F * (rank + 1)]).then_inc(sem.c_b, 1)
     V.wait_ge(sem.c_a, 1)
     V.wait_ge(sem.a1_0, 4)
-    V.tensor_tensor(T.accA[:, 0:2 * F], T.accA[:, 0:2 * F], T.l1[:, 0:2 * F], add).then_inc(sem.r1a, 1)
-    V.wait_ge(sem.r1a, 1)
+    V.tensor_tensor(T.tb[:, :], T.accA[:, 0:2 * F], T.l1[:, 0:2 * F], add).then_inc(sem.r1a, 1)
     V.wait_ge(sem.a1_1, 4)
-    V.tensor_tensor(T.accA[:, 0:2 * F], T.accA[:, 0:2 * F], T.l1[:, 2 * F:4 * F], add).then_inc(sem.r1b, 1)
-    V.wait_ge(sem.r1b, 1)
     V.wait_ge(sem.a1_2, 4)
-    V.tensor_tensor(T.r1[:, :], T.accA[:, 0:2 * F], T.l1[:, 4 * F:6 * F], add).then_inc(sem.r1done, 1)
+    V.tensor_tensor(T.accA[:, 2 * F:4 * F], T.l1[:, 2 * F:4 * F], T.l1[:, 4 * F:6 * F], add).then_inc(sem.r1b, 1)
+    V.wait_ge(sem.r1a, 1)
+    V.wait_ge(sem.r1b, 1)
+    V.tensor_tensor(T.r1[:, :], T.accA[:, 2 * F:4 * F], T.tb[:, :], add).then_inc(sem.r1done, 1)
 
     g.wait_ge(sem.r1done, 1)
     trs = []
@@ -191,45 +188,20 @@ def rank_program(g, core, T, topo):
 
     P = g.tensor
     g.wait_ge(sem.sq, 1)
-    if S3_FLAT:
-        def slot_at(c):
-            return (rank - cores.index(c) - 1) % n_ranks
-        trs = [RemoteDMATransfer(dst_ids=[dst_id(c) for c in far], dma_engine_mask=_bits(e_off), remote_sem=sem.a3,
-                                 srcs=[T.qown[:, 0:1]], dsts=[T.qland[:, slot_at(c):slot_at(c) + 1] for c in far]),
-               RemoteDMATransfer(dst_ids=[dst_id(c) for c in sibs], dma_engine_mask=_bits(e_rest), remote_sem=sem.a3,
-                                 srcs=[T.qown[:, 0:1]], dsts=[T.qland[:, slot_at(c):slot_at(c) + 1] for c in sibs])]
-        lsem_total += len(e_off) + len(e_rest)
-        g.remote_dma_fused(trs, local_sem=sem.lsem)
-        P.wait_ge(sem.m_ones, 1)
-        P.wait_ge(sem.sq, 1)
-        P.matmul(T.ps[:, 0:1], T.ones[:, :], T.qown[:, 0:1], True, True).then_inc(sem.pe0, 1)
-        P.wait_ge(sem.a3, len(e_off) * len(far) + len(e_rest) * len(sibs))
-        P.matmul(T.ps[:, 1:ncol], T.ones[:, :], T.qland[:, 0:ncol - 1], True, True).then_inc(sem.pe1, 1)
-    else:
-        ns = len(sibs)
-        trs = [RemoteDMATransfer(dst_ids=[dst_id(c) for c in sibs], dma_engine_mask=_bits(e_on), remote_sem=sem.a3,
-                                 srcs=[T.qown[:, 0:1]],
-                                 dsts=[T.qland[:, siblings(c).index(core):siblings(c).index(core) + 1] for c in sibs])]
-        lsem_total += len(e_on)
-        g.remote_dma_fused(trs, local_sem=sem.lsem)
-        V.wait_ge(sem.m_zr, 1)
-        V.wait_ge(sem.sq, 1)
-        V.wait_ge(sem.a3, len(e_on) * ns)
-        V.tensor_tensor_scan(T.qchip[:, 0:ns], T.qland[:, 0:ns], T.zr[:, 0:ns], T.qown[:, 0:1], add, add
-                             ).then_inc(sem.qcs, 1)
-        peers = [members[ch][members[mychip].index(core)] for ch in oth]
-        g.wait_ge(sem.qcs, 1)
-        trs = [RemoteDMATransfer(dst_ids=[dst_id(c) for c in peers], dma_engine_mask=_bits(e_off), remote_sem=sem.a4,
-                                 srcs=[T.qchip[:, ns - 1:ns]],
-                                 dsts=[T.qland2[:, others(topo.chip(c)).index(mychip):
-                                                others(topo.chip(c)).index(mychip) + 1] for c in peers])]
-        lsem_total += len(e_off)
-        g.remote_dma_fused(trs, local_sem=sem.lsem)
-        P.wait_ge(sem.m_ones, 1)
-        P.wait_ge(sem.qcs, 1)
-        P.matmul(T.ps[:, 0:1], T.ones[:, :], T.qchip[:, ns - 1:ns], True, True).then_inc(sem.pe0, 1)
-        P.wait_ge(sem.a4, len(e_off) * len(peers))
-        P.matmul(T.ps[:, 1:ncol], T.ones[:, :], T.qland2[:, 0:ncol - 1], True, True).then_inc(sem.pe1, 1)
+
+    def slot_at(c):
+        return (rank - cores.index(c) - 1) % n_ranks
+    trs = [RemoteDMATransfer(dst_ids=[dst_id(c) for c in far], dma_engine_mask=_bits(e_off), remote_sem=sem.a3,
+                             srcs=[T.qown[:, 0:1]], dsts=[T.qland[:, slot_at(c):slot_at(c) + 1] for c in far]),
+           RemoteDMATransfer(dst_ids=[dst_id(c) for c in sibs], dma_engine_mask=_bits(e_rest), remote_sem=sem.a3,
+                             srcs=[T.qown[:, 0:1]], dsts=[T.qland[:, slot_at(c):slot_at(c) + 1] for c in sibs])]
+    lsem_total += len(e_off) + len(e_rest)
+    g.remote_dma_fused(trs, local_sem=sem.lsem)
+    P.wait_ge(sem.m_ones, 1)
+    P.wait_ge(sem.sq, 1)
+    P.matmul(T.ps[:, 0:1], T.ones[:, :], T.qown[:, 0:1], True, True).then_inc(sem.pe0, 1)
+    P.wait_ge(sem.a3, len(e_off) * len(far) + len(e_rest) * len(sibs))
+    P.matmul(T.ps[:, 1:ncol], T.ones[:, :], T.qland[:, 0:ncol - 1], True, True).then_inc(sem.pe1, 1)
 
     V.wait_ge(sem.m_flr, 2)
     V.wait_ge(sem.pe0, 1)
@@ -237,15 +209,18 @@ def rank_program(g, core, T, topo):
     V.tensor_tensor_scan(T.scn[:, 0:ncol], T.ps[:, 0:ncol], T.flr[:, 0:ncol], 0.0, add, mx).then_inc(sem.qc, 1)
     qc = T.scn[:, ncol - 1:ncol]
     g.scalar.wait_ge(sem.qc, 1)
-    g.scalar.activation(T.z[:, 0:1], qc, ActivationFunctionType.Sqrt).then_inc(sem.zs, 1)
+    g.scalar.activation(T.zb[:, 0:1], qc, ActivationFunctionType.Sqrt).then_inc(sem.zs, 1)
+    V.wait_ge(sem.qc, 1)
+    V.reciprocal(T.rq[:, 0:1], qc).then_inc(sem.rqs, 1)
+    V.wait_ge(sem.rqs, 1)
+    V.tensor_scalar(T.zb[:, 1:2], T.rq[:, 0:1], -0.5, None, mult).then_inc(sem.h1, 1)
+    V.tensor_scalar(T.zb[:, 2:3], T.rq[:, 0:1], kk, None, mult).then_inc(sem.h1, 1)
+    V.wait_ge(sem.h1, 2)
+    V.wait_ge(sem.m_d1, 3)
     V.wait_ge(sem.zs, 1)
-    V.reciprocal(T.rz[:, 0:1], T.z[:, 0:1]).then_inc(sem.rzs, 1)
-    V.wait_ge(sem.rzs, 1)
-    V.tensor_scalar(T.t[:, 0:1], T.rz[:, 0:1], T.rz[:, 0:1], qc, mult, mult).then_inc(sem.ts, 1)
-    V.wait_ge(sem.ts, 1)
-    V.tensor_scalar(T.u[:, 0:1], T.t[:, 0:1], -0.5 * kk, 1.5 * kk, mult, add).then_inc(sem.us, 1)
-    V.wait_ge(sem.us, 1)
-    V.tensor_scalar(T.ysb[:, :], T.s[:, :], T.rz[:, 0:1], T.u[:, 0:1], mult, mult).then_inc(sem.ydone, 1)
+    V.tensor_tensor_scan(T.sc2[:, 0:3], T.zb[:, 0:3], T.d1[:, 0:3], T.zb[:, 0:1], mult, add).then_inc(sem.s2s, 1)
+    V.wait_ge(sem.s2s, 1)
+    V.tensor_scalar(T.ysb[:, :], T.s[:, :], T.sc2[:, 2:3], T.zb[:, 0:1], mult, mult).then_inc(sem.ydone, 1)
 
     g.sync.wait_ge(sem.ydone, 1)
     g.sync.dma_start(T.y[:, :], T.ysb[:, :]).then_inc(sem.st, 16)

@@ -19,16 +19,17 @@ SCRATCH = {
     "scn": ("sbuf", [128, 12], "float32"),
     "rq": ("sbuf", [128, 4], "float32"),
     "zb": ("sbuf", [128, 4], "float32"),
-    "d1": ("sbuf", [128, 4], "float32"),
-    "sc2": ("sbuf", [128, 4], "float32"),
+    "seed": ("sbuf", [128, 4], "float32"),
+    "acol": ("sbuf", [128, 4], "float32"),
+    "ab": ("sbuf", [128, 4], "float32"),
     "ysb": ("sbuf", [128, 64], "float32"),
     "accA": ("psum", [128, 512], "float32"),
     "accB": ("psum", [128, 512], "float32"),
     "ps": ("psum", [128, 512], "float32"),
 }
 SEMAPHORES = ["ld0", "ld1", "ld2", "a1_0", "a1_1", "a1_2", "b1", "a2_0", "a2_1", "a3", "lsem",
-              "m_ones", "m_flr", "m_d1", "c_a", "c_b", "r1a", "r1b", "r1done", "bb0", "bb1", "bb2", "r2a", "sdone",
-              "sq", "pe0", "pe1", "qc", "zs", "rqs", "h1", "s2s", "ydone", "st"]
+              "m_ones", "m_flr", "m_seed", "asem", "abs1", "c_a", "c_b", "r1a", "r1b", "r1done", "bb0", "bb1", "bb2",
+              "r2a", "sdone", "sq", "pe0", "pe1", "qc", "zs", "rqs", "ydone", "st"]
 
 
 def _engines(mask):
@@ -102,17 +103,14 @@ def rank_program(g, core, T, topo):
     g.sync.dma_start(T.x[:, a:b], T.gr[:, a:b]).then_inc(sem.ld2, 16)
 
     bound = float(T.tables["BOUND"])
-    sg = 2.0 ** -39
-    kk = sg * bound
-    floor = kk * kk
+    phi = 2.0 ** -25
     ncol = n_ranks
     V = g.vector
+    V.memset(T.seed[:, 0:1], phi / (bound * bound)).then_inc(sem.m_seed, 1)
     V.memset(T.ones[:, :], 1.0).then_inc(sem.m_ones, 1)
     V.memset(T.flr[:, 0:ncol - 1], 0.0).then_inc(sem.m_flr, 1)
-    V.memset(T.flr[:, ncol - 1:ncol], floor).then_inc(sem.m_flr, 1)
-    V.memset(T.d1[:, 0:1], 0.0).then_inc(sem.m_d1, 1)
-    V.memset(T.d1[:, 1:2], 1.5).then_inc(sem.m_d1, 1)
-    V.memset(T.d1[:, 2:3], 0.0).then_inc(sem.m_d1, 1)
+    g.scalar.wait_ge(sem.m_seed, 1)
+    g.scalar.activation(T.acol[:, 0:1], T.seed[:, 0:1], ActivationFunctionType.Sqrt).then_inc(sem.asem, 1)
 
     lsem_total = 0
 
@@ -155,6 +153,11 @@ def rank_program(g, core, T, topo):
     V.wait_ge(sem.r1b, 1)
     V.tensor_tensor(T.r1[:, :], T.accA[:, 2 * F:4 * F], T.tb[:, :], add).then_inc(sem.r1done, 1)
 
+    V.wait_ge(sem.asem, 1)
+    V.tensor_scalar(T.ab[:, 0:1], T.acol[:, 0:1], bound, None, mult).then_inc(sem.abs1, 1)
+    V.wait_ge(sem.abs1, 1)
+    V.tensor_tensor(T.flr[:, ncol - 1:ncol], T.ab[:, 0:1], T.ab[:, 0:1], mult).then_inc(sem.m_flr, 1)
+
     g.wait_ge(sem.r1done, 1)
     trs = []
     for j, r in enumerate(mypair):
@@ -182,8 +185,9 @@ def rank_program(g, core, T, topo):
     V.wait_ge(sem.a2_1, 4)
     V.tensor_tensor(T.s[:, :], T.accB[:, 0:F], T.l2[:, F:2 * F], add).then_inc(sem.sdone, 1)
 
+    g.scalar.wait_ge(sem.asem, 1)
     g.scalar.wait_ge(sem.sdone, 1)
-    g.scalar.activation(T.sqj[:, :], T.s[:, :], ActivationFunctionType.Square, scale=sg,
+    g.scalar.activation(T.sqj[:, :], T.s[:, :], ActivationFunctionType.Square, scale=T.acol[:, 0:1],
                         accum_out=T.qown[:, 0:1]).then_inc(sem.sq, 1)
 
     P = g.tensor
@@ -207,20 +211,16 @@ def rank_program(g, core, T, topo):
     V.wait_ge(sem.pe0, 1)
     V.wait_ge(sem.pe1, 1)
     V.tensor_tensor_scan(T.scn[:, 0:ncol], T.ps[:, 0:ncol], T.flr[:, 0:ncol], 0.0, add, mx).then_inc(sem.qc, 1)
-    qc = T.scn[:, ncol - 1:ncol]
+    w = T.scn[:, ncol - 1:ncol]
+    g.scalar.wait_ge(sem.m_flr, 2)
     g.scalar.wait_ge(sem.qc, 1)
-    g.scalar.activation(T.zb[:, 0:1], qc, ActivationFunctionType.Sqrt).then_inc(sem.zs, 1)
+    g.scalar.activation(T.zb[:, 0:1], w, ActivationFunctionType.Sqrt,
+                        scale=T.flr[:, ncol - 1:ncol]).then_inc(sem.zs, 1)
     V.wait_ge(sem.qc, 1)
-    V.reciprocal(T.rq[:, 0:1], qc).then_inc(sem.rqs, 1)
+    V.reciprocal(T.rq[:, 0:1], w).then_inc(sem.rqs, 1)
     V.wait_ge(sem.rqs, 1)
-    V.tensor_scalar(T.zb[:, 1:2], T.rq[:, 0:1], -0.5, None, mult).then_inc(sem.h1, 1)
-    V.tensor_scalar(T.zb[:, 2:3], T.rq[:, 0:1], kk, None, mult).then_inc(sem.h1, 1)
-    V.wait_ge(sem.h1, 2)
-    V.wait_ge(sem.m_d1, 3)
     V.wait_ge(sem.zs, 1)
-    V.tensor_tensor_scan(T.sc2[:, 0:3], T.zb[:, 0:3], T.d1[:, 0:3], T.zb[:, 0:1], mult, add).then_inc(sem.s2s, 1)
-    V.wait_ge(sem.s2s, 1)
-    V.tensor_scalar(T.ysb[:, :], T.s[:, :], T.sc2[:, 2:3], T.zb[:, 0:1], mult, mult).then_inc(sem.ydone, 1)
+    V.tensor_scalar(T.ysb[:, :], T.s[:, :], T.rq[:, 0:1], T.zb[:, 0:1], mult, mult).then_inc(sem.ydone, 1)
 
     g.sync.wait_ge(sem.ydone, 1)
     g.sync.dma_start(T.y[:, :], T.ysb[:, :]).then_inc(sem.st, 16)

from concourse.bass import DstId, RemoteDMATransfer
from concourse.mybir import AluOpType, ActivationFunctionType

F = 64

SCRATCH = {
    "x": ("sbuf", [128, 768], "float32"),
    "l1": ("sbuf", [128, 384], "float32"),
    "lb": ("sbuf", [128, 192], "float32"),
    "l2": ("sbuf", [128, 128], "float32"),
    "tb": ("sbuf", [128, 128], "float32"),
    "r1": ("sbuf", [128, 128], "float32"),
    "s": ("sbuf", [128, 64], "float32"),
    "sqj": ("sbuf", [128, 64], "float32"),
    "qown": ("sbuf", [128, 4], "float32"),
    "qland": ("sbuf", [128, 12], "float32"),
    "ones": ("sbuf", [128, 128], "float32"),
    "flr": ("sbuf", [128, 12], "float32"),
    "scn": ("sbuf", [128, 12], "float32"),
    "rq": ("sbuf", [128, 4], "float32"),
    "zb": ("sbuf", [128, 4], "float32"),
    "seed": ("sbuf", [128, 4], "float32"),
    "acol": ("sbuf", [128, 4], "float32"),
    "ab": ("sbuf", [128, 4], "float32"),
    "ysb": ("sbuf", [128, 64], "float32"),
    "accA": ("psum", [128, 512], "float32"),
    "accB": ("psum", [128, 512], "float32"),
    "ps": ("psum", [128, 512], "float32"),
}
SEMAPHORES = ["ld0", "ld1", "ld2", "a1_0", "a1_1", "a1_2", "b1", "a2_0", "a2_1", "a3", "lsem",
              "m_ones", "m_flr", "m_seed", "asem", "abs1", "c_a", "c_b", "r1a", "r1b", "r1done", "bb0", "bb1", "bb2",
              "r2a", "sdone", "sq", "pe0", "pe1", "qc", "zs", "rqs", "ydone", "st"]


def _engines(mask):
    return [e for e in range(mask.bit_length()) if (mask >> e) & 1]


def _bits(es):
    m = 0
    for e in es:
        m |= 1 << e
    return m


def rank_program(g, core, T, topo):
    rank = T.rank_of(core)
    if rank is None:
        return
    cores = list(T.cores)
    n_ranks = len(cores)
    sem = T.sem
    add, mult, mx = AluOpType.add, AluOpType.mult, AluOpType.max

    chips = []
    for c in cores:
        if topo.chip(c) not in chips:
            chips.append(topo.chip(c))
    members = {ch: [c for c in cores if topo.chip(c) == ch] for ch in chips}

    def others(ch):
        i = chips.index(ch)
        return [chips[(i + k) % len(chips)] for k in range(1, len(chips))]

    def siblings(c):
        return [m for m in members[topo.chip(c)] if m != c]

    def pair(c):
        d = topo.die(c)
        same = [m for m in members[topo.chip(c)] if topo.die(m) == d]
        xch = others(topo.chip(c))[same.index(c)]
        rs = [cores.index(m) for m in members[xch] if topo.die(m) == d]
        assert len(rs) == 2 and rs[1] == rs[0] + 1
        return rs

    def group_cols(ch):
        rs = [cores.index(m) for m in members[ch]]
        assert rs == list(range(rs[0], rs[0] + len(rs)))
        return F * rs[0], F * (rs[-1] + 1)

    def dst_id(c):
        assert topo.may_write(core, c)
        rid, pid, _ = topo.addr(c)
        return DstId(rid=rid, pnc=pid)

    mychip = topo.chip(core)
    sibs = siblings(core)
    oth = others(mychip)
    far = [c for c in cores if topo.chip(c) != mychip]
    e_on = _engines(topo.mask(core, sibs[0]))
    e_off = _engines(topo.mask(core, far[0]))
    e_rest = [e for e in e_on if e not in e_off]
    s1b_groups = [e_rest[0:4], e_rest[4:6], e_rest[6:8]]
    mypair = pair(core)
    pc0 = F * mypair[0]

    lds = [sem.ld0, sem.ld1, sem.ld2]
    a, b = group_cols(oth[0])
    g.sync.dma_start(T.x[:, a:b], T.gr[:, a:b]).then_inc(sem.ld0, 16)
    a, b = group_cols(oth[1])
    g.scalar.dma_start(T.x[:, a:b], T.gr[:, a:b]).then_inc(sem.ld1, 16)
    a, b = group_cols(mychip)
    g.sync.dma_start(T.x[:, a:b], T.gr[:, a:b]).then_inc(sem.ld2, 16)

    bound = float(T.tables["BOUND"])
    phi = 2.0 ** -25
    ncol = n_ranks
    V = g.vector
    V.memset(T.seed[:, 0:1], phi / (bound * bound)).then_inc(sem.m_seed, 1)
    V.memset(T.ones[:, :], 1.0).then_inc(sem.m_ones, 1)
    V.memset(T.flr[:, 0:ncol - 1], 0.0).then_inc(sem.m_flr, 1)
    g.scalar.wait_ge(sem.m_seed, 1)
    g.scalar.activation(T.acol[:, 0:1], T.seed[:, 0:1], ActivationFunctionType.Sqrt).then_inc(sem.asem, 1)

    lsem_total = 0

    g.wait_ge(sem.ld0, 16)
    g.wait_ge(sem.ld1, 16)
    trs = []
    for j, h in enumerate(sibs):
        p0 = F * pair(h)[0]
        slot = siblings(h).index(core)
        es = e_on[4 * j:4 * j + 4]
        trs.append(RemoteDMATransfer(dst_ids=[dst_id(h)], dma_engine_mask=_bits(es),
                                     remote_sem=sem["a1_%d" % slot],
                                     src=T.x[:, p0:p0 + 2 * F], dst=T.l1[:, 2 * F * slot:2 * F * (slot + 1)]))
        lsem_total += len(es)
    g.remote_dma_fused(trs, local_sem=sem.lsem)

    g.wait_ge(sem.ld2, 16)
    trs = []
    for j, h in enumerate(sibs):
        c0 = F * cores.index(h)
        slot = siblings(h).index(core)
        es = s1b_groups[j]
        trs.append(RemoteDMATransfer(dst_ids=[dst_id(h)], dma_engine_mask=_bits(es), remote_sem=sem.b1,
                                     src=T.x[:, c0:c0 + F], dst=T.lb[:, F * slot:F * (slot + 1)]))
        lsem_total += len(es)
    g.remote_dma_fused(trs, local_sem=sem.lsem)
    b1_total = sum(len(s1b_groups[siblings(h).index(core)]) for h in sibs)

    V.wait_ge(lds[oth.index(topo.chip(cores[mypair[0]]))], 16)
    V.tensor_copy(T.accA[:, 0:2 * F], T.x[:, pc0:pc0 + 2 * F]).then_inc(sem.c_a, 1)
    V.wait_ge(sem.ld2, 16)
    V.tensor_copy(T.accB[:, 0:F], T.x[:, F * rank:F * (rank + 1)]).then_inc(sem.c_b, 1)
    V.wait_ge(sem.c_a, 1)
    V.wait_ge(sem.a1_0, 4)
    V.tensor_tensor(T.tb[:, :], T.accA[:, 0:2 * F], T.l1[:, 0:2 * F], add).then_inc(sem.r1a, 1)
    V.wait_ge(sem.a1_1, 4)
    V.wait_ge(sem.a1_2, 4)
    V.tensor_tensor(T.accA[:, 2 * F:4 * F], T.l1[:, 2 * F:4 * F], T.l1[:, 4 * F:6 * F], add).then_inc(sem.r1b, 1)
    V.wait_ge(sem.r1a, 1)
    V.wait_ge(sem.r1b, 1)
    V.tensor_tensor(T.r1[:, :], T.accA[:, 2 * F:4 * F], T.tb[:, :], add).then_inc(sem.r1done, 1)

    V.wait_ge(sem.asem, 1)
    V.tensor_scalar(T.ab[:, 0:1], T.acol[:, 0:1], bound, None, mult).then_inc(sem.abs1, 1)
    V.wait_ge(sem.abs1, 1)
    V.tensor_tensor(T.flr[:, ncol - 1:ncol], T.ab[:, 0:1], T.ab[:, 0:1], mult).then_inc(sem.m_flr, 1)

    g.wait_ge(sem.r1done, 1)
    trs = []
    for j, r in enumerate(mypair):
        o = cores[r]
        slot = others(topo.chip(o)).index(mychip)
        es = e_off[4 * j:4 * j + 4]
        trs.append(RemoteDMATransfer(dst_ids=[dst_id(o)], dma_engine_mask=_bits(es),
                                     remote_sem=sem["a2_%d" % slot],
                                     src=T.r1[:, F * j:F * (j + 1)], dst=T.l2[:, F * slot:F * (slot + 1)]))
        lsem_total += len(es)
    g.remote_dma_fused(trs, local_sem=sem.lsem)

    V.wait_ge(sem.c_b, 1)
    V.wait_ge(sem.b1, b1_total)
    prev = None
    for k, sm in enumerate([sem.bb0, sem.bb1, sem.bb2]):
        if prev is not None:
            V.wait_ge(prev, 1)
        V.tensor_tensor(T.accB[:, 0:F], T.accB[:, 0:F], T.lb[:, F * k:F * (k + 1)], add).then_inc(sm, 1)
        prev = sm
    V.wait_ge(sem.bb2, 1)
    V.wait_ge(sem.a2_0, 4)
    V.tensor_tensor(T.accB[:, 0:F], T.accB[:, 0:F], T.l2[:, 0:F], add).then_inc(sem.r2a, 1)
    V.wait_ge(sem.r2a, 1)
    V.wait_ge(sem.a2_1, 4)
    V.tensor_tensor(T.s[:, :], T.accB[:, 0:F], T.l2[:, F:2 * F], add).then_inc(sem.sdone, 1)

    g.scalar.wait_ge(sem.asem, 1)
    g.scalar.wait_ge(sem.sdone, 1)
    g.scalar.activation(T.sqj[:, :], T.s[:, :], ActivationFunctionType.Square, scale=T.acol[:, 0:1],
                        accum_out=T.qown[:, 0:1]).then_inc(sem.sq, 1)

    P = g.tensor
    g.wait_ge(sem.sq, 1)

    def slot_at(c):
        return (rank - cores.index(c) - 1) % n_ranks
    trs = [RemoteDMATransfer(dst_ids=[dst_id(c) for c in far], dma_engine_mask=_bits(e_off), remote_sem=sem.a3,
                             srcs=[T.qown[:, 0:1]], dsts=[T.qland[:, slot_at(c):slot_at(c) + 1] for c in far]),
           RemoteDMATransfer(dst_ids=[dst_id(c) for c in sibs], dma_engine_mask=_bits(e_rest), remote_sem=sem.a3,
                             srcs=[T.qown[:, 0:1]], dsts=[T.qland[:, slot_at(c):slot_at(c) + 1] for c in sibs])]
    lsem_total += len(e_off) + len(e_rest)
    g.remote_dma_fused(trs, local_sem=sem.lsem)
    P.wait_ge(sem.m_ones, 1)
    P.wait_ge(sem.sq, 1)
    P.matmul(T.ps[:, 0:1], T.ones[:, :], T.qown[:, 0:1], True, True).then_inc(sem.pe0, 1)
    P.wait_ge(sem.a3, len(e_off) * len(far) + len(e_rest) * len(sibs))
    P.matmul(T.ps[:, 1:ncol], T.ones[:, :], T.qland[:, 0:ncol - 1], True, True).then_inc(sem.pe1, 1)

    V.wait_ge(sem.m_flr, 2)
    V.wait_ge(sem.pe0, 1)
    V.wait_ge(sem.pe1, 1)
    V.tensor_tensor_scan(T.scn[:, 0:ncol], T.ps[:, 0:ncol], T.flr[:, 0:ncol], 0.0, add, mx).then_inc(sem.qc, 1)
    w = T.scn[:, ncol - 1:ncol]
    g.scalar.wait_ge(sem.m_flr, 2)
    g.scalar.wait_ge(sem.qc, 1)
    g.scalar.activation(T.zb[:, 0:1], w, ActivationFunctionType.Sqrt,
                        scale=T.flr[:, ncol - 1:ncol]).then_inc(sem.zs, 1)
    V.wait_ge(sem.qc, 1)
    V.reciprocal(T.rq[:, 0:1], w).then_inc(sem.rqs, 1)
    V.wait_ge(sem.rqs, 1)
    V.wait_ge(sem.zs, 1)
    V.tensor_scalar(T.ysb[:, :], T.s[:, :], T.rq[:, 0:1], T.zb[:, 0:1], mult, mult).then_inc(sem.ydone, 1)

    g.sync.wait_ge(sem.ydone, 1)
    g.sync.dma_start(T.y[:, :], T.ysb[:, :]).then_inc(sem.st, 16)
    g.sync.wait_ge(sem.st, 16)
    g.wait_ge(sem.lsem, lsem_total)
